import numpy as np
import ml_dtypes


def mxq(x, axis, fmt="e4m3"):
    dtype, down = {"e4m3": (ml_dtypes.float8_e4m3fn, 7), "e5m2": (ml_dtypes.float8_e5m2, 14)}[fmt]
    v = np.moveaxis(np.asarray(x, np.float32).astype(ml_dtypes.bfloat16).astype(np.float64), axis, -1)
    blocks = v.reshape(v.shape[:-1] + (-1, 32))
    amax = np.abs(blocks).max(-1, keepdims=True)
    byte = np.maximum(np.where(amax > 0, np.frexp(amax)[1] - 1 + 127, 0) - down, 1)
    scale = np.exp2(byte - 127.0)
    codes = (blocks / scale).astype(np.float32).astype(dtype).astype(np.float64)
    return np.moveaxis((codes * scale).reshape(v.shape), -1, axis)


WIDE = False


def mx_kscale(k):
    if not WIDE:
        return np.ones(k)
    levels = np.array([10, -10, 5, -5, 0])
    if k % 512:
        return np.exp2(np.random.permutation(np.resize(levels, k // 32))).repeat(32)
    a = np.empty((k // 512, 16))
    for p in range(k // 512):
        a[p, :8] = np.random.permutation(np.resize(levels, 8))
        for g in range(8):
            far = levels[np.abs(levels - a[p, g]) >= 10]
            a[p, g + 8] = far[np.random.randint(len(far))]
    return np.exp2(a.ravel()).repeat(32)


def f64(x):
    return np.asarray(x).astype(np.float64)


def striped(idx):
    return np.tile(idx.reshape(-1, 16).T, (8, 1)).astype(np.uint16)


def unstriped(offs):
    return offs[:16].T.reshape(-1).astype(np.int64)


E2M1 = np.array([0.0, 0.5, 1.0, 1.5, 2.0, 3.0, 4.0, 6.0, -0.0, -0.5, -1.0, -1.5, -2.0, -3.0, -4.0, -6.0])


def pack_weight(w, fmt):
    k, n = w.shape
    w = f64(np.asarray(w, np.float32).astype(ml_dtypes.bfloat16)).reshape(k // 32, 32, n)
    amax = np.abs(w).max(1)
    if fmt == "e4m3":
        byte = np.frexp(amax)[1] - 1 + 127 - 7
    else:
        mant, ex = np.frexp(amax / 6.0)
        byte = np.where(mant > 0.5, ex, ex - 1) + 127
    byte = np.clip(np.where(amax > 0, byte, 1), 1, 254)
    scaled = (w * np.exp2(127.0 - byte)[:, None, :]).reshape(k, n).astype(np.float32)
    by_word = np.ascontiguousarray(scaled.reshape(k // 512, 128, 4, n).transpose(0, 1, 3, 2))
    if fmt == "e4m3":
        words = by_word.astype(ml_dtypes.float8_e4m3fn).view(np.uint8)
    else:
        c = by_word.astype(ml_dtypes.float4_e2m1fn).view(np.uint8) & 0xF
        words = (c[..., 0::2] | (c[..., 1::2] << 4)).reshape(k // 512, 128, 2 * n)
    return np.ascontiguousarray(words), np.ascontiguousarray(byte.astype(np.uint8).reshape(k // 512, 16, n))


def unpack_weight(words, scales, fmt):
    g, _, n = scales.shape
    words = np.ascontiguousarray(words).reshape(g, 128, n, -1)
    if fmt == "e4m3":
        vals = words.view(ml_dtypes.float8_e4m3fn).astype(np.float64)
    else:
        nib = np.empty((g, 128, n, 4), np.uint8)
        nib[..., 0::2] = words & 0xF
        nib[..., 1::2] = words >> 4
        vals = E2M1[nib]
    vals = vals * np.repeat(np.exp2(scales.astype(np.float64) - 127.0), 8, axis=1)[..., None]
    return vals.transpose(0, 1, 3, 2).reshape(g * 512, n)


def gelu(v):
    return 0.5 * v * (1.0 + np.tanh(np.sqrt(2.0 / np.pi) * (v + 0.044715 * v**3)))


K, H, T, S, T2, T3, S2 = 1024, 1024, 4096, 1024, 2048, 2048, 512

def setup_inputs():
    n = np.random.standard_normal
    s = mx_kscale(K)[:, None]
    u = mx_kscale(H)[:, None]
    tab_words, tab_scales = pack_weight(n((K, T)) * s, "e4m3")
    tab2_words, tab2_scales = pack_weight(n((H, T3)) / u / np.sqrt(H), "e4m3")
    w4_words, w4_scales = pack_weight(0.8 * n((K, H)) / s * u.T / np.sqrt(K), "e2m1")
    return {
        "tab_words": tab_words, "tab_scales": tab_scales,
        "offs": striped(np.random.permutation(T)[:S]),
        "w1": (1.6 * n((K, H)) / s / np.sqrt(K)).astype(np.float32),
        "gain": (1.3 * np.exp(0.3 * n(H)) * u[:, 0]).astype(np.float32),
        "w4_words": w4_words, "w4_scales": w4_scales,
        "tab2_words": tab2_words, "tab2_scales": tab2_scales,
        "offs2": striped(np.random.permutation(T3)[:S2]),
        "aw": np.exp(0.4 * n(S2)).astype(np.float32),
        "prior": (0.8 * n((S2, S))).astype(np.float32),
        "page1": n((S2, T2)).astype(np.float32),
        "wgo": np.exp(0.3 * n((128, S))).astype(np.float32),
        "offs3": striped(np.random.permutation(T2)[:S]),
    }

def reference(tab_words, tab_scales, offs, w1, gain, w4_words, w4_scales,
              tab2_words, tab2_scales, offs2, aw, prior, page1, wgo, offs3):
    v = unpack_weight(tab_words, tab_scales, "e4m3")[:, unstriped(offs)]
    v2 = unpack_weight(tab2_words, tab2_scales, "e4m3")[:, unstriped(offs2)]
    w4 = unpack_weight(w4_words, w4_scales, "e2m1")
    bent = np.tanh(mxq(f64(w1), 0, "e4m3").T @ v)
    h = f64(gain)[:, None] * bent + (w4.T @ v)
    hq = mxq(h, 0, "e4m3")
    e = v2.T @ hq
    marks = f64(aw)[:, None] * e + f64(prior)
    out = f64(page1).copy()
    out[:, unstriped(offs3)] = np.tile(f64(wgo), (S2 // 128, 1)) * marks
    return out

@@ -1,0 +1,253 @@
+from contextlib import ExitStack
+
+import concourse.mybir as mybir
+
+K, H, T, S, T2, T3, S2 = 1024, 1024, 4096, 1024, 2048, 2048, 512
+FLOPS = 2 * (2 * K * H * S + H * S2 * S)
+
+F32 = mybir.dt.float32
+BF16 = mybir.dt.bfloat16
+I32 = mybir.dt.int32
+U32 = mybir.dt.uint32
+U16 = mybir.dt.uint16
+U8 = mybir.dt.uint8
+FP8X4 = mybir.dt.float8_e4m3fn_x4
+FP4X4 = mybir.dt.float4_e2m1fn_x4
+ALU = mybir.AluOpType
+ACT = mybir.ActivationFunctionType
+
+P = 128
+PACK = 4
+KP = P * PACK
+NJ = 512
+W1_VECTOR_SHARE = 80
+H_VECTOR_SHARE = 256
+
+
+def tile_list_essay_mark_moderation_kernel(
+    tc, tab_words, tab_scales, offs, w1, gain, w4_words, w4_scales,
+    tab2_words, tab2_scales, offs2, aw, prior, page1, wgo, offs3, out,
+):
+    nc = tc.nc
+    passes = K // KP
+    halves = S // NJ
+    row_tiles = S2 // P
+    list_cols = NJ // 16
+
+    with ExitStack() as ctx:
+        keep = ctx.enter_context(tc.tile_pool(name="keep", bufs=1))
+        ring = ctx.enter_context(tc.tile_pool(name="ring", bufs=1))
+        psum = ctx.enter_context(tc.psum_pool(name="psum", bufs=4))
+
+        idx = keep.tile([P, S // 16], U16, name="idx")
+        idx2 = keep.tile([P, S2 // 16], U16, name="idx2")
+        idx3 = keep.tile([P, S // 16], U16, name="idx3")
+
+        tab_sc = keep.tile([P, passes, T], U8, name="tab_sc", align_bytes=64)
+        w4_sc_raw = keep.tile([P, passes, H], U8, name="w4_sc_raw", align_bytes=64)
+        tab2_sc = keep.tile([P, T3], U8, name="tab2_sc", align_bytes=64)
+        nc.vector.memset(tab_sc[:, 0, :].bitcast(I32), 0)
+        nc.gpsimd.memset(tab_sc[:, 1, :].bitcast(I32), 0)
+        nc.vector.memset(w4_sc_raw[:].bitcast(I32), 0)
+        nc.vector.memset(tab2_sc[:].bitcast(I32), 0)
+        tab_rows = tab_scales.bitcast(I32).rearrange("a (q r) t -> r q a t", r=4)
+        w4_rows = w4_scales.bitcast(I32).rearrange("a (q r) t -> r q a t", r=4)
+
+        nc.sync.dma_start(idx[:], offs)
+        gain_sb = keep.tile([P, passes, PACK], F32, name="gain_sb")
+        nc.sync.dma_start(out=gain_sb[:], in_=gain.rearrange("(b p t) -> p b t", p=P, t=PACK))
+        nc.sync.dma_start(idx2[:], offs2)
+        nc.sync.dma_start(idx3[:], offs3)
+        aw_sb = keep.tile([P, row_tiles], F32, name="aw_sb")
+        with nc.allow_non_contiguous_dma(reason="one anchor weight for each partition and row tile"):
+            nc.sync.dma_start(out=aw_sb[:], in_=aw.rearrange("(c p) -> p c", p=P))
+        w4_raw = keep.tile([P, passes, 2 * H], U8, name="w4_raw", align_bytes=64)
+        nc.sync.dma_start(out=w4_raw[:].bitcast(I32), in_=w4_words.bitcast(I32).rearrange("a p c -> p a c"))
+        for r in range(4):
+            nc.sync.dma_start(out=tab_sc[r:P:32].bitcast(I32), in_=tab_rows[r])
+        tab_w = []
+        for a in range(passes):
+            tw = keep.tile([P, T], I32, name=f"tab_w{a}", align_bytes=64)
+            nc.sync.dma_start(out=tw[:], in_=tab_words[a].rearrange("p t i -> p (t i)").bitcast(I32))
+            tab_w.append(tw)
+            if a == 0:
+                for r in range(4):
+                    nc.sync.dma_start(out=w4_sc_raw[r:P:32].bitcast(I32), in_=w4_rows[r])
+        w1_raw = {}
+        for b in range(passes):
+            for a in range(passes):
+                raw = ring.tile([P, PACK, KP], F32, name=f"w1_raw{b}{a}", tag="raw", bufs=4)
+                nc.sync.dma_start(
+                    out=raw[:],
+                    in_=w1[a * KP : (a + 1) * KP, b * KP : (b + 1) * KP].rearrange("(p i) c -> p i c", i=PACK),
+                )
+                w1_raw[b, a] = raw
+        for q in range(4):
+            nc.sync.dma_start(
+                out=tab2_sc[32 * q : 32 * q + 4 * passes, :].bitcast(I32),
+                in_=tab2_scales.bitcast(I32)[:, 4 * q : 4 * q + 4, :],
+            )
+        tab2_w = []
+        for b in range(passes):
+            tw = keep.tile([P, T3], I32, name=f"tab2_w{b}", align_bytes=64)
+            nc.sync.dma_start(out=tw[:], in_=tab2_words[b].rearrange("p t i -> p (t i)").bitcast(I32))
+            tab2_w.append(tw)
+        wgo_sb = [keep.tile([P, NJ], F32, name=f"wgo{jh}") for jh in range(halves)]
+        nc.sync.dma_start(out=wgo_sb[0][:], in_=wgo[:, 0:NJ])
+        prior_sb = {}
+        pages = []
+        for c in range(row_tiles):
+            pr = keep.tile([P, NJ], F32, name=f"prior{c}")
+            nc.sync.dma_start(out=pr[:], in_=prior[c * P : (c + 1) * P, 0:NJ])
+            prior_sb[c, 0] = pr[:]
+            page = keep.tile([P, T2], F32, name=f"page{c}")
+            nc.sync.dma_start(out=page[:], in_=page1[c * P : (c + 1) * P, :])
+            pages.append(page)
+        nc.sync.dma_start(out=wgo_sb[1][:], in_=wgo[:, NJ : 2 * NJ])
+
+        w4_w = keep.tile([P, passes, 2 * H], U8, name="w4_w", align_bytes=64)
+        w4_sc = keep.tile([P, passes, H], U8, name="w4_sc", align_bytes=64)
+        nc.scalar.copy(
+            out=w4_w[:].bitcast(U16).rearrange("p a (b t m) -> p (a b) m t", t=PACK, m=P),
+            in_=w4_raw[:].bitcast(U16).rearrange("p a (b m t) -> p (a b) m t", t=PACK, m=P),
+        )
+        nc.vector.tensor_copy(
+            out=w4_sc[:].rearrange("p a (b t m) -> p (a b) t m", t=PACK, m=P),
+            in_=w4_sc_raw[:].rearrange("p a (b m t) -> p (a b) t m", t=PACK, m=P),
+        )
+
+        v_w, v_sc = {}, {}
+
+        def gather_scripts(jh):
+            cut = idx[:, jh * list_cols : (jh + 1) * list_cols]
+            for a in range(passes):
+                sc = keep.tile([P, NJ], U8, name=f"v_sc{a}{jh}", align_bytes=64)
+                nc.vector.tensor_copy(out=sc[:], in_=tab_sc[:, a, :].indirect(cut))
+                v_sc[a, jh] = sc
+            for a in range(passes):
+                words = keep.tile([P, NJ], U32, name=f"v_w{a}{jh}", align_bytes=64)
+                nc.vector.tensor_copy(out=words[:], in_=tab_w[a][:].bitcast(U32).indirect(cut))
+                v_w[a, jh] = words
+
+        w1_w, w1_sc = {}, {}
+
+        def quantize_w1(b, a):
+            grouped = ring.tile([P, PACK, P, PACK], BF16, name="w1_grouped", tag="w1g", bufs=2, align_bytes=64)
+            dst = grouped[:].rearrange("p t m i -> p m i t")
+            src = w1_raw[b, a][:].rearrange("p i (m t) -> p m i t", t=PACK)
+            nc.vector.tensor_copy(out=dst[:, 0:W1_VECTOR_SHARE], in_=src[:, 0:W1_VECTOR_SHARE])
+            nc.scalar.copy(out=dst[:, W1_VECTOR_SHARE:P], in_=src[:, W1_VECTOR_SHARE:P])
+            words = keep.tile([P, KP], U32, name=f"w1_w{b}{a}", align_bytes=64)
+            sc = keep.tile([P, KP], U8, name=f"w1_sc{b}{a}", align_bytes=64)
+            nc.vector.quantize_mx(
+                out=words[:].bitcast(FP8X4), scales=sc[:], in_=grouped[:].rearrange("p t m i -> p (t m i)")
+            )
+            w1_w[b, a], w1_sc[b, a] = words, sc
+
+        h_w, h_sc = {}, {}
+
+        def features(b, jh, vector_cols):
+            planes = ring.tile([P, PACK, NJ], BF16, name="h_planes", tag="hp", bufs=3, align_bytes=64)
+            for t in range(PACK):
+                lin = psum.tile([P, NJ], F32, name="lin", tag="lin")
+                for a in range(passes):
+                    c0 = b * KP + t * P
+                    nc.tensor.matmul_mx(
+                        out=lin[:],
+                        lhsT=w4_w[:, a, 2 * c0 : 2 * (c0 + P)].bitcast(FP4X4),
+                        lhsT_scale=w4_sc[:, a, c0 : c0 + P],
+                        rhs=v_w[a, jh][:].bitcast(FP8X4),
+                        rhs_scale=v_sc[a, jh][:],
+                        start=(a == 0), stop=(a == passes - 1),
+                    )
+                pre = psum.tile([P, NJ], F32, name="pre", tag="acc")
+                for a in range(passes):
+                    nc.tensor.matmul_mx(
+                        out=pre[:],
+                        lhsT=w1_w[b, a][:, t * P : (t + 1) * P].bitcast(FP8X4),
+                        lhsT_scale=w1_sc[b, a][:, t * P : (t + 1) * P],
+                        rhs=v_w[a, jh][:].bitcast(FP8X4),
+                        rhs_scale=v_sc[a, jh][:],
+                        start=(a == 0), stop=(a == passes - 1),
+                    )
+                bent = ring.tile([P, NJ], F32, name="bent", tag="bent", bufs=6)
+                nc.scalar.activation(out=bent[:], in_=pre[:], func=ACT.Tanh)
+                nc.vector.scalar_tensor_tensor(
+                    out=planes[:, t, :], in0=bent[:], scalar=gain_sb[:, b, t : t + 1], in1=lin[:],
+                    op0=ALU.mult, op1=ALU.add,
+                )
+            woven = ring.tile([P, NJ, PACK], BF16, name="h_woven", tag="hw", bufs=2, align_bytes=64)
+            dst = woven[:].rearrange("p (g n) t -> p g t n", n=4)
+            src = planes[:].rearrange("p t (g n) -> p g t n", n=4)
+            cut = vector_cols // 4
+            if cut > 0:
+                nc.vector.tensor_copy(out=dst[:, 0:cut], in_=src[:, 0:cut])
+            nc.scalar.copy(out=dst[:, cut : NJ // 4], in_=src[:, cut : NJ // 4])
+            words = keep.tile([P, NJ], U32, name=f"h_w{b}{jh}", align_bytes=64)
+            sc = keep.tile([P, NJ], U8, name=f"h_sc{b}{jh}", align_bytes=64)
+            nc.vector.quantize_mx(
+                out=words[:].bitcast(FP8X4), scales=sc[:], in_=woven[:].rearrange("p n t -> p (n t)")
+            )
+            h_w[b, jh], h_sc[b, jh] = words, sc
+
+        v2_w = []
+        v2_sc = keep.tile([P, S2], U8, name="v2_sc", align_bytes=64)
+
+        def gather_anchors():
+            nc.vector.tensor_copy(out=v2_sc[:], in_=tab2_sc[:].indirect(idx2[:]))
+            for b in range(passes):
+                words = keep.tile([P, S2], U32, name=f"v2_w{b}", align_bytes=64)
+                nc.vector.tensor_copy(out=words[:], in_=tab2_w[b][:].bitcast(U32).indirect(idx2[:]))
+                v2_w.append(words)
+
+        marks = {}
+
+        def score(c, jh):
+            e = psum.tile([P, NJ], F32, name="e", tag="acc")
+            for b in range(passes):
+                nc.tensor.matmul_mx(
+                    out=e[:],
+                    lhsT=v2_w[b][:, c * P : (c + 1) * P].bitcast(FP8X4),
+                    lhsT_scale=v2_sc[4 * b : P, c * P : (c + 1) * P],
+                    rhs=h_w[b, jh][:].bitcast(FP8X4),
+                    rhs_scale=h_sc[b, jh][:],
+                    start=(b == 0), stop=(b == passes - 1),
+                )
+            mk = ring.tile([P, NJ], F32, name="marks", tag="marks", bufs=3)
+            nc.vector.scalar_tensor_tensor(
+                out=mk[:], in0=e[:], scalar=aw_sb[:, c : c + 1], in1=prior_sb[c, jh],
+                op0=ALU.mult, op1=ALU.add,
+            )
+            marks[c, jh] = mk
+
+        def put(c, jh):
+            cut = idx3[:, jh * list_cols : (jh + 1) * list_cols]
+            nc.vector.tensor_tensor(
+                out=pages[c][:].indirect(cut), in0=marks[c, jh][:], in1=wgo_sb[jh][:], op=ALU.mult
+            )
+            if jh == halves - 1:
+                nc.sync.dma_start(out=out[c * P : (c + 1) * P, :], in_=pages[c][:])
+
+        gather_scripts(0)
+        quantize_w1(0, 0)
+        quantize_w1(0, 1)
+        features(0, 0, 0)
+        quantize_w1(1, 0)
+        quantize_w1(1, 1)
+        prior_late = ring.tile([P, row_tiles, NJ], F32, name="prior_late", tag="raw", bufs=4)
+        nc.sync.dma_start(out=prior_late[:], in_=prior[:, NJ : 2 * NJ].rearrange("(c p) n -> p c n", p=P))
+        for c in range(row_tiles):
+            prior_sb[c, 1] = prior_late[:, c, :]
+        gather_scripts(1)
+        features(1, 0, H_VECTOR_SHARE)
+        gather_anchors()
+        score(0, 0)
+        features(0, 1, 0)
+        score(1, 0)
+        put(0, 0)
+        features(1, 1, 0)
+        order = [(c, jh) for jh in range(halves) for c in range(row_tiles)]
+        for n in range(1, len(order)):
+            if n + 1 < len(order):
+                score(*order[n + 1])
+            put(*order[n])

@@ -1,6 +1,7 @@
 from contextlib import ExitStack
 
 import concourse.mybir as mybir
+from concourse.masks import make_identity
 
 K, H, T, S, T2, T3, S2 = 1024, 1024, 4096, 1024, 2048, 2048, 512
 FLOPS = 2 * (2 * K * H * S + H * S2 * S)
@@ -21,7 +22,7 @@ PACK = 4
 KP = P * PACK
 NJ = 512
 W1_VECTOR_SHARE = 80
-H_VECTOR_SHARE = 256
+H_VECTOR_SHARE = 320
 
 
 def tile_list_essay_mark_moderation_kernel(
@@ -37,17 +38,25 @@ def tile_list_essay_mark_moderation_kernel(
     with ExitStack() as ctx:
         keep = ctx.enter_context(tc.tile_pool(name="keep", bufs=1))
         ring = ctx.enter_context(tc.tile_pool(name="ring", bufs=1))
-        psum = ctx.enter_context(tc.psum_pool(name="psum", bufs=4))
+        psum = ctx.enter_context(tc.psum_pool(name="psum", bufs=1))
 
         idx = keep.tile([P, S // 16], U16, name="idx")
         idx2 = keep.tile([P, S2 // 16], U16, name="idx2")
         idx3 = keep.tile([P, S // 16], U16, name="idx3")
 
-        tab_sc = keep.tile([P, passes, T], U8, name="tab_sc", align_bytes=64)
+        def slot(shape, dtype, name, tag):
+            return ring.tile(shape, dtype, name=name, tag=tag, bufs=1, align_bytes=64)
+
+        def bank(n, name):
+            return psum.tile([P, NJ], F32, name=name, tag=f"bank{n}")
+
+        tab_sc = keep.tile([P, T], U8, name="tab_sc", align_bytes=64)
         w4_sc_raw = keep.tile([P, passes, H], U8, name="w4_sc_raw", align_bytes=64)
         tab2_sc = keep.tile([P, T3], U8, name="tab2_sc", align_bytes=64)
-        nc.vector.memset(tab_sc[:, 0, :].bitcast(I32), 0)
-        nc.gpsimd.memset(tab_sc[:, 1, :].bitcast(I32), 0)
+        v_sc_moved = keep.tile([P, S], U8, name="v_sc_moved", align_bytes=64)
+        nc.vector.memset(tab_sc[:, 0 : T // 2].bitcast(I32), 0)
+        nc.gpsimd.memset(tab_sc[:, T // 2 : T].bitcast(I32), 0)
+        nc.gpsimd.memset(v_sc_moved[:].bitcast(I32), 0)
         nc.vector.memset(w4_sc_raw[:].bitcast(I32), 0)
         nc.vector.memset(tab2_sc[:].bitcast(I32), 0)
         tab_rows = tab_scales.bitcast(I32).rearrange("a (q r) t -> r q a t", r=4)
@@ -56,55 +65,66 @@ def tile_list_essay_mark_moderation_kernel(
         nc.sync.dma_start(idx[:], offs)
         gain_sb = keep.tile([P, passes, PACK], F32, name="gain_sb")
         nc.sync.dma_start(out=gain_sb[:], in_=gain.rearrange("(b p t) -> p b t", p=P, t=PACK))
-        nc.sync.dma_start(idx2[:], offs2)
-        nc.sync.dma_start(idx3[:], offs3)
-        aw_sb = keep.tile([P, row_tiles], F32, name="aw_sb")
-        with nc.allow_non_contiguous_dma(reason="one anchor weight for each partition and row tile"):
-            nc.sync.dma_start(out=aw_sb[:], in_=aw.rearrange("(c p) -> p c", p=P))
         w4_raw = keep.tile([P, passes, 2 * H], U8, name="w4_raw", align_bytes=64)
         nc.sync.dma_start(out=w4_raw[:].bitcast(I32), in_=w4_words.bitcast(I32).rearrange("a p c -> p a c"))
         for r in range(4):
-            nc.sync.dma_start(out=tab_sc[r:P:32].bitcast(I32), in_=tab_rows[r])
-        tab_w = []
-        for a in range(passes):
-            tw = keep.tile([P, T], I32, name=f"tab_w{a}", align_bytes=64)
-            nc.sync.dma_start(out=tw[:], in_=tab_words[a].rearrange("p t i -> p (t i)").bitcast(I32))
-            tab_w.append(tw)
-            if a == 0:
-                for r in range(4):
-                    nc.sync.dma_start(out=w4_sc_raw[r:P:32].bitcast(I32), in_=w4_rows[r])
+            nc.sync.dma_start(out=tab_sc[r:P:16].bitcast(I32), in_=tab_rows[r])
+        tab_w = [keep.tile([P, T], I32, name=f"tab_w{a}", align_bytes=64) for a in range(passes)]
+        tab_src = [tab_words[a].rearrange("p t i -> p (t i)").bitcast(I32) for a in range(passes)]
+        nc.sync.dma_start(out=tab_w[0][:, 0 : T // 2], in_=tab_src[0][:, 0 : T // 2])
+        for r in range(4):
+            nc.sync.dma_start(out=w4_sc_raw[r:P:32].bitcast(I32), in_=w4_rows[r])
+        nc.sync.dma_start(idx2[:], offs2)
+        nc.sync.dma_start(out=tab_w[0][:, T // 2 : T], in_=tab_src[0][:, T // 2 : T])
+        for q in range(4):
+            nc.sync.dma_start(
+                out=tab2_sc[32 * q + 8 : 32 * q + 16, :].bitcast(I32),
+                in_=tab2_scales.bitcast(I32)[:, 4 * q : 4 * q + 4, :],
+            )
+        nc.sync.dma_start(out=tab_w[1][:], in_=tab_src[1])
         w1_raw = {}
         for b in range(passes):
             for a in range(passes):
-                raw = ring.tile([P, PACK, KP], F32, name=f"w1_raw{b}{a}", tag="raw", bufs=4)
+                raw = slot([P, PACK, KP], F32, f"w1_raw{b}{a}", f"raw{b}{a}")
                 nc.sync.dma_start(
                     out=raw[:],
                     in_=w1[a * KP : (a + 1) * KP, b * KP : (b + 1) * KP].rearrange("(p i) c -> p i c", i=PACK),
                 )
                 w1_raw[b, a] = raw
-        for q in range(4):
-            nc.sync.dma_start(
-                out=tab2_sc[32 * q : 32 * q + 4 * passes, :].bitcast(I32),
-                in_=tab2_scales.bitcast(I32)[:, 4 * q : 4 * q + 4, :],
-            )
         tab2_w = []
         for b in range(passes):
-            tw = keep.tile([P, T3], I32, name=f"tab2_w{b}", align_bytes=64)
+            tw = slot([P, T3], I32, f"tab2_w{b}", f"tab2_w{b}")
             nc.sync.dma_start(out=tw[:], in_=tab2_words[b].rearrange("p t i -> p (t i)").bitcast(I32))
             tab2_w.append(tw)
+        nc.sync.dma_start(idx3[:], offs3)
+        aw_sb = keep.tile([P, row_tiles], F32, name="aw_sb")
+        with nc.allow_non_contiguous_dma(reason="one anchor weight for each partition and row tile"):
+            nc.sync.dma_start(out=aw_sb[:], in_=aw.rearrange("(c p) -> p c", p=P))
         wgo_sb = [keep.tile([P, NJ], F32, name=f"wgo{jh}") for jh in range(halves)]
         nc.sync.dma_start(out=wgo_sb[0][:], in_=wgo[:, 0:NJ])
         prior_sb = {}
+
+        def load_prior(jh, tag):
+            pr = slot([P, row_tiles, NJ], F32, f"prior{jh}", tag)
+            nc.sync.dma_start(
+                out=pr[:], in_=prior[:, jh * NJ : (jh + 1) * NJ].rearrange("(c p) n -> p c n", p=P)
+            )
+            prior_sb[jh] = pr
+
+        load_prior(0, "prior0")
         pages = []
         for c in range(row_tiles):
-            pr = keep.tile([P, NJ], F32, name=f"prior{c}")
-            nc.sync.dma_start(out=pr[:], in_=prior[c * P : (c + 1) * P, 0:NJ])
-            prior_sb[c, 0] = pr[:]
             page = keep.tile([P, T2], F32, name=f"page{c}")
             nc.sync.dma_start(out=page[:], in_=page1[c * P : (c + 1) * P, :])
             pages.append(page)
         nc.sync.dma_start(out=wgo_sb[1][:], in_=wgo[:, NJ : 2 * NJ])
 
+        ident = keep.tile([P, P], F32, name="ident")
+        make_identity(nc, ident[:])
+
+        v_sc_packed = keep.tile([P, S], U8, name="v_sc_packed", align_bytes=64)
+        nc.vector.tensor_copy(out=v_sc_packed[:], in_=tab_sc[:].indirect(idx[:]))
+        nc.gpsimd.dma_start(out=v_sc_moved[0 : P - 16, :].bitcast(I32), in_=v_sc_packed[16:P, :].bitcast(I32))
         w4_w = keep.tile([P, passes, 2 * H], U8, name="w4_w", align_bytes=64)
         w4_sc = keep.tile([P, passes, H], U8, name="w4_sc", align_bytes=64)
         nc.scalar.copy(
@@ -116,14 +136,14 @@ def tile_list_essay_mark_moderation_kernel(
             in_=w4_sc_raw[:].rearrange("p a (b m t) -> p (a b) t m", t=PACK, m=P),
         )
 
-        v_w, v_sc = {}, {}
+        v_w = {}
+        v_sc = {
+            (a, jh): (v_sc_packed, v_sc_moved)[a][:, jh * NJ : (jh + 1) * NJ]
+            for a in range(passes) for jh in range(halves)
+        }
 
         def gather_scripts(jh):
             cut = idx[:, jh * list_cols : (jh + 1) * list_cols]
-            for a in range(passes):
-                sc = keep.tile([P, NJ], U8, name=f"v_sc{a}{jh}", align_bytes=64)
-                nc.vector.tensor_copy(out=sc[:], in_=tab_sc[:, a, :].indirect(cut))
-                v_sc[a, jh] = sc
             for a in range(passes):
                 words = keep.tile([P, NJ], U32, name=f"v_w{a}{jh}", align_bytes=64)
                 nc.vector.tensor_copy(out=words[:], in_=tab_w[a][:].bitcast(U32).indirect(cut))
@@ -131,12 +151,12 @@ def tile_list_essay_mark_moderation_kernel(
 
         w1_w, w1_sc = {}, {}
 
-        def quantize_w1(b, a):
-            grouped = ring.tile([P, PACK, P, PACK], BF16, name="w1_grouped", tag="w1g", bufs=2, align_bytes=64)
+        def quantize_w1(b, a, share):
+            grouped = slot([P, PACK, P, PACK], BF16, f"w1_grouped{b}{a}", f"grouped{a}")
             dst = grouped[:].rearrange("p t m i -> p m i t")
             src = w1_raw[b, a][:].rearrange("p i (m t) -> p m i t", t=PACK)
-            nc.vector.tensor_copy(out=dst[:, 0:W1_VECTOR_SHARE], in_=src[:, 0:W1_VECTOR_SHARE])
-            nc.scalar.copy(out=dst[:, W1_VECTOR_SHARE:P], in_=src[:, W1_VECTOR_SHARE:P])
+            nc.vector.tensor_copy(out=dst[:, 0:share], in_=src[:, 0:share])
+            nc.scalar.copy(out=dst[:, share:P], in_=src[:, share:P])
             words = keep.tile([P, KP], U32, name=f"w1_w{b}{a}", align_bytes=64)
             sc = keep.tile([P, KP], U8, name=f"w1_sc{b}{a}", align_bytes=64)
             nc.vector.quantize_mx(
@@ -144,57 +164,72 @@ def tile_list_essay_mark_moderation_kernel(
             )
             w1_w[b, a], w1_sc[b, a] = words, sc
 
-        h_w, h_sc = {}, {}
-
-        def features(b, jh, vector_cols):
-            planes = ring.tile([P, PACK, NJ], BF16, name="h_planes", tag="hp", bufs=3, align_bytes=64)
-            for t in range(PACK):
-                lin = psum.tile([P, NJ], F32, name="lin", tag="lin")
-                for a in range(passes):
-                    c0 = b * KP + t * P
-                    nc.tensor.matmul_mx(
-                        out=lin[:],
-                        lhsT=w4_w[:, a, 2 * c0 : 2 * (c0 + P)].bitcast(FP4X4),
-                        lhsT_scale=w4_sc[:, a, c0 : c0 + P],
-                        rhs=v_w[a, jh][:].bitcast(FP8X4),
-                        rhs_scale=v_sc[a, jh][:],
-                        start=(a == 0), stop=(a == passes - 1),
-                    )
-                pre = psum.tile([P, NJ], F32, name="pre", tag="acc")
-                for a in range(passes):
-                    nc.tensor.matmul_mx(
-                        out=pre[:],
-                        lhsT=w1_w[b, a][:, t * P : (t + 1) * P].bitcast(FP8X4),
-                        lhsT_scale=w1_sc[b, a][:, t * P : (t + 1) * P],
-                        rhs=v_w[a, jh][:].bitcast(FP8X4),
-                        rhs_scale=v_sc[a, jh][:],
-                        start=(a == 0), stop=(a == passes - 1),
-                    )
-                bent = ring.tile([P, NJ], F32, name="bent", tag="bent", bufs=6)
-                nc.scalar.activation(out=bent[:], in_=pre[:], func=ACT.Tanh)
-                nc.vector.scalar_tensor_tensor(
-                    out=planes[:, t, :], in0=bent[:], scalar=gain_sb[:, b, t : t + 1], in1=lin[:],
-                    op0=ALU.mult, op1=ALU.add,
+        def linear(b, jh, t, n):
+            lin = bank(n, f"lin{b}{jh}")
+            c0 = b * KP + t * P
+            for a in range(passes):
+                nc.tensor.matmul_mx(
+                    out=lin[:],
+                    lhsT=w4_w[:, a, 2 * c0 : 2 * (c0 + P)].bitcast(FP4X4),
+                    lhsT_scale=w4_sc[:, a, c0 : c0 + P],
+                    rhs=v_w[a, jh][:].bitcast(FP8X4),
+                    rhs_scale=v_sc[a, jh],
+                    start=(a == 0), stop=(a == passes - 1),
                 )
-            woven = ring.tile([P, NJ, PACK], BF16, name="h_woven", tag="hw", bufs=2, align_bytes=64)
-            dst = woven[:].rearrange("p (g n) t -> p g t n", n=4)
+            return lin
+
+        def bend(b, jh, t, n, bent):
+            pre = bank(n, f"pre{b}{jh}")
+            for a in range(passes):
+                nc.tensor.matmul_mx(
+                    out=pre[:],
+                    lhsT=w1_w[b, a][:, t * P : (t + 1) * P].bitcast(FP8X4),
+                    lhsT_scale=w1_sc[b, a][:, t * P : (t + 1) * P],
+                    rhs=v_w[a, jh][:].bitcast(FP8X4),
+                    rhs_scale=v_sc[a, jh],
+                    start=(a == 0), stop=(a == passes - 1),
+                )
+            nc.scalar.activation(out=bent, in_=pre[:], func=ACT.Tanh)
+
+        def join(b, t, planes, bent, lin):
+            nc.vector.scalar_tensor_tensor(
+                out=planes[:, t, :], in0=bent, scalar=gain_sb[:, b, t : t + 1], in1=lin[:],
+                op0=ALU.mult, op1=ALU.add,
+            )
+
+        def weave(planes, woven, vector_cols):
+            dst = woven.rearrange("p (g n) t -> p g t n", n=4)
             src = planes[:].rearrange("p t (g n) -> p g t n", n=4)
             cut = vector_cols // 4
             if cut > 0:
                 nc.vector.tensor_copy(out=dst[:, 0:cut], in_=src[:, 0:cut])
-            nc.scalar.copy(out=dst[:, cut : NJ // 4], in_=src[:, cut : NJ // 4])
-            words = keep.tile([P, NJ], U32, name=f"h_w{b}{jh}", align_bytes=64)
-            sc = keep.tile([P, NJ], U8, name=f"h_sc{b}{jh}", align_bytes=64)
-            nc.vector.quantize_mx(
-                out=words[:].bitcast(FP8X4), scales=sc[:], in_=woven[:].rearrange("p n t -> p (n t)")
-            )
-            h_w[b, jh], h_sc[b, jh] = words, sc
+                nc.scalar.copy(out=dst[:, cut : NJ // 4], in_=src[:, cut : NJ // 4])
+            else:
+                nc.scalar.copy(out=dst[:, 0 : NJ // 8], in_=src[:, 0 : NJ // 8])
+                nc.scalar.copy(out=dst[:, NJ // 8 : NJ // 4], in_=src[:, NJ // 8 : NJ // 4])
+
+        h_w, h_sc = {}, {}
+
+        def quantize_h(jh, wovens, tag, whole=None):
+            words = slot([P, passes, NJ], U32, f"h_w{jh}", tag)
+            sc = keep.tile([P, passes, NJ], U8, name=f"h_sc{jh}", align_bytes=64)
+            if whole is not None:
+                nc.vector.quantize_mx(
+                    out=words[:].rearrange("p b n -> p (b n)").bitcast(FP8X4),
+                    scales=sc[:].rearrange("p b n -> p (b n)"),
+                    in_=whole[:].rearrange("p b n t -> p (b n t)"),
+                )
+            for b in range(passes if whole is None else 0):
+                nc.vector.quantize_mx(
+                    out=words[:, b, :].bitcast(FP8X4), scales=sc[:, b, :],
+                    in_=wovens[b][:].rearrange("p n t -> p (n t)"),
+                )
+            h_w[jh], h_sc[jh] = words, sc
 
         v2_w = []
         v2_sc = keep.tile([P, S2], U8, name="v2_sc", align_bytes=64)
 
         def gather_anchors():
-            nc.vector.tensor_copy(out=v2_sc[:], in_=tab2_sc[:].indirect(idx2[:]))
             for b in range(passes):
                 words = keep.tile([P, S2], U32, name=f"v2_w{b}", align_bytes=64)
                 nc.vector.tensor_copy(out=words[:], in_=tab2_w[b][:].bitcast(U32).indirect(idx2[:]))
@@ -202,22 +237,49 @@ def tile_list_essay_mark_moderation_kernel(
 
         marks = {}
 
-        def score(c, jh):
-            e = psum.tile([P, NJ], F32, name="e", tag="acc")
+        def match(c, jh, n):
+            e = bank(n, f"e{c}{jh}")
             for b in range(passes):
                 nc.tensor.matmul_mx(
                     out=e[:],
                     lhsT=v2_w[b][:, c * P : (c + 1) * P].bitcast(FP8X4),
-                    lhsT_scale=v2_sc[4 * b : P, c * P : (c + 1) * P],
-                    rhs=h_w[b, jh][:].bitcast(FP8X4),
-                    rhs_scale=h_sc[b, jh][:],
+                    lhsT_scale=v2_sc[8 + 4 * b : P, c * P : (c + 1) * P],
+                    rhs=h_w[jh][:, b, :].bitcast(FP8X4),
+                    rhs_scale=h_sc[jh][:, b, :],
                     start=(b == 0), stop=(b == passes - 1),
                 )
-            mk = ring.tile([P, NJ], F32, name="marks", tag="marks", bufs=3)
+            return e
+
+        def score_on_vector(c, jh, e, tag):
+            mk = slot([P, NJ], F32, f"marks{c}{jh}", tag)
             nc.vector.scalar_tensor_tensor(
-                out=mk[:], in0=e[:], scalar=aw_sb[:, c : c + 1], in1=prior_sb[c, jh],
+                out=mk[:], in0=e[:], scalar=aw_sb[:, c : c + 1], in1=prior_sb[jh][:, c, :],
                 op0=ALU.mult, op1=ALU.add,
             )
+            marks[c, jh] = mk
+
+        def score_on_tensor(c, jh, banks):
+            e = match(c, jh, banks[0])
+            scaled = slot([P, NJ], F32, f"scaled{c}{jh}", f"scaled{c % 2}")
+            nc.scalar.activation(out=scaled[:], in_=e[:], func=ACT.Copy, scale=aw_sb[:, c : c + 1])
+            turned = bank(banks[1], f"turned{c}{jh}")
+            for g in range(NJ // P):
+                cols = slice(g * P, (g + 1) * P)
+                nc.tensor.matmul(turned[:, cols], lhsT=prior_sb[jh][:, c, cols], rhs=ident[:],
+                                 is_transpose=True, start=True, stop=False)
+                nc.tensor.matmul(turned[:, cols], lhsT=scaled[:, cols], rhs=ident[:],
+                                 is_transpose=True, start=False, stop=True)
+            summed = slot([P, NJ], F32, f"summed{c}{jh}", f"summed{c % 2}")
+            nc.scalar.copy(out=summed[:], in_=turned[:])
+            back = bank(banks[2], f"back{c}{jh}")
+            for g in range(NJ // P):
+                cols = slice(g * P, (g + 1) * P)
+                nc.tensor.transpose(back[:, cols], summed[:, cols], ident[:])
+            return back
+
+        def fetch_marks(c, jh, back, tag):
+            mk = slot([P, NJ], F32, f"marks{c}{jh}", tag)
+            nc.scalar.copy(out=mk[:], in_=back[:])
             marks[c, jh] = mk
 
         def put(c, jh):
@@ -229,25 +291,65 @@ def tile_list_essay_mark_moderation_kernel(
                 nc.sync.dma_start(out=out[c * P : (c + 1) * P, :], in_=pages[c][:])
 
         gather_scripts(0)
-        quantize_w1(0, 0)
-        quantize_w1(0, 1)
-        features(0, 0, 0)
-        quantize_w1(1, 0)
-        quantize_w1(1, 1)
-        prior_late = ring.tile([P, row_tiles, NJ], F32, name="prior_late", tag="raw", bufs=4)
-        nc.sync.dma_start(out=prior_late[:], in_=prior[:, NJ : 2 * NJ].rearrange("(c p) n -> p c n", p=P))
-        for c in range(row_tiles):
-            prior_sb[c, 1] = prior_late[:, c, :]
         gather_scripts(1)
-        features(1, 0, H_VECTOR_SHARE)
+        nc.vector.tensor_copy(out=v2_sc[:], in_=tab2_sc[:].indirect(idx2[:]))
+        lin00 = [linear(0, 0, t, t) for t in range(PACK)]
+        quantize_w1(0, 0, 80)
+        quantize_w1(0, 1, 80)
+        quantize_w1(1, 0, 80)
+        load_prior(1, "raw01")
+        planes00 = slot([P, PACK, NJ], BF16, "planes00", "planes0")
+        bent = slot([P, PACK, NJ], F32, "bent00", "raw10")
+        for t in range(PACK):
+            bend(0, 0, t, 4 + t, bent[:, t, :])
+            join(0, t, planes00, bent[:, t, :], lin00[t])
+        lin10 = [linear(1, 0, t, t) for t in range(PACK)]
+        quantize_w1(1, 1, 80)
+        woven00 = slot([P, NJ, PACK], BF16, "woven00", "grouped0")
+        weave(planes00, woven00[:], 0)
         gather_anchors()
-        score(0, 0)
-        features(0, 1, 0)
-        score(1, 0)
+        planes10 = slot([P, PACK, NJ], BF16, "planes10", "tab2_w1")
+        bent = slot([P, PACK, NJ], F32, "bent10", "raw00")
+        for t in range(PACK):
+            bend(1, 0, t, 4 + t, bent[:, t, :])
+            join(1, t, planes10, bent[:, t, :], lin10[t])
+        woven10 = slot([P, NJ, PACK], BF16, "woven10", "grouped1")
+        weave(planes10, woven10[:], H_VECTOR_SHARE)
+        quantize_h(0, [woven00, woven10], "raw00")
+
+        bent01 = slot([P, PACK, NJ], F32, "bent01", "tab2_w1")
+        lin01 = [linear(0, 1, t, t) for t in range(PACK)]
+        for t in range(PACK):
+            bend(0, 1, t, 4 + t, bent01[:, t, :])
+        score_on_vector(0, 0, match(0, 0, 4), "marks0")
+        e10 = match(1, 0, 5)
+        bent11 = slot([P, PACK, NJ], F32, "bent11", "raw10")
+        for t in range(PACK):
+            bend(1, 1, t, 6 + t % 2, bent11[:, t, :])
+        back20 = score_on_tensor(2, 0, (4, 6, 7))
+        planes01 = slot([P, PACK, NJ], BF16, "planes01", "grouped1")
+        for t in range(PACK):
+            join(0, t, planes01, bent01[:, t, :], lin01[t])
+        lin11 = [linear(1, 1, t, t) for t in range(PACK)]
         put(0, 0)
-        features(1, 1, 0)
-        order = [(c, jh) for jh in range(halves) for c in range(row_tiles)]
-        for n in range(1, len(order)):
-            if n + 1 < len(order):
-                score(*order[n + 1])
-            put(*order[n])
+        woven1 = slot([P, passes, NJ, PACK], BF16, "woven1", "tab2_w0")
+        weave(planes01, woven1[:, 0], 0)
+        planes11 = slot([P, PACK, NJ], BF16, "planes11", "marks0")
+        for t in range(PACK):
+            join(1, t, planes11, bent11[:, t, :], lin11[t])
+        score_on_vector(1, 0, e10, "raw10")
+        put(1, 0)
+        weave(planes11, woven1[:, 1], 0)
+        fetch_marks(2, 0, back20, "marks0")
+        quantize_h(1, None, "raw10", woven1)
+        fetch_marks(3, 0, score_on_tensor(3, 0, (0, 1, 2)), "marks3")
+        put(2, 0)
+        put(3, 0)
+        score_on_vector(0, 1, match(0, 1, 5), "marks3")
+        fetch_marks(1, 1, score_on_tensor(1, 1, (3, 4, 6)), "raw11")
+        put(0, 1)
+        fetch_marks(2, 1, score_on_tensor(2, 1, (4, 0, 1)), "grouped0")
+        put(1, 1)
+        fetch_marks(3, 1, score_on_tensor(3, 1, (0, 3, 6)), "planes0")
+        put(2, 1)
+        put(3, 1)

@@ -64,7 +64,7 @@ def tile_list_essay_mark_moderation_kernel(
 
         nc.sync.dma_start(idx[:], offs)
         gain_sb = keep.tile([P, passes, PACK], F32, name="gain_sb")
-        nc.sync.dma_start(out=gain_sb[:], in_=gain.rearrange("(b p t) -> p b t", p=P, t=PACK))
+        nc.sync.dma_start(idx2[:], offs2)
         w4_raw = keep.tile([P, passes, 2 * H], U8, name="w4_raw", align_bytes=64)
         nc.sync.dma_start(out=w4_raw[:].bitcast(I32), in_=w4_words.bitcast(I32).rearrange("a p c -> p a c"))
         for r in range(4):
@@ -74,7 +74,6 @@ def tile_list_essay_mark_moderation_kernel(
         nc.sync.dma_start(out=tab_w[0][:, 0 : T // 2], in_=tab_src[0][:, 0 : T // 2])
         for r in range(4):
             nc.sync.dma_start(out=w4_sc_raw[r:P:32].bitcast(I32), in_=w4_rows[r])
-        nc.sync.dma_start(idx2[:], offs2)
         nc.sync.dma_start(out=tab_w[0][:, T // 2 : T], in_=tab_src[0][:, T // 2 : T])
         for q in range(4):
             nc.sync.dma_start(
@@ -82,6 +81,7 @@ def tile_list_essay_mark_moderation_kernel(
                 in_=tab2_scales.bitcast(I32)[:, 4 * q : 4 * q + 4, :],
             )
         nc.sync.dma_start(out=tab_w[1][:], in_=tab_src[1])
+        nc.sync.dma_start(out=gain_sb[:], in_=gain.rearrange("(b p t) -> p b t", p=P, t=PACK))
         w1_raw = {}
         for b in range(passes):
             for a in range(passes):
@@ -127,10 +127,10 @@ def tile_list_essay_mark_moderation_kernel(
         nc.gpsimd.dma_start(out=v_sc_moved[0 : P - 16, :].bitcast(I32), in_=v_sc_packed[16:P, :].bitcast(I32))
         w4_w = keep.tile([P, passes, 2 * H], U8, name="w4_w", align_bytes=64)
         w4_sc = keep.tile([P, passes, H], U8, name="w4_sc", align_bytes=64)
-        nc.scalar.copy(
-            out=w4_w[:].bitcast(U16).rearrange("p a (b t m) -> p (a b) m t", t=PACK, m=P),
-            in_=w4_raw[:].bitcast(U16).rearrange("p a (b m t) -> p (a b) m t", t=PACK, m=P),
-        )
+        w4_dst = w4_w[:].bitcast(U16).rearrange("p a (b t m) -> p (a b) m t", t=PACK, m=P)
+        w4_src = w4_raw[:].bitcast(U16).rearrange("p a (b m t) -> p (a b) m t", t=PACK, m=P)
+        for t in range(0, PACK, 2):
+            nc.scalar.copy(out=w4_dst[:, :, :, t : t + 2], in_=w4_src[:, :, :, t : t + 2])
         nc.vector.tensor_copy(
             out=w4_sc[:].rearrange("p a (b t m) -> p (a b) t m", t=PACK, m=P),
             in_=w4_sc_raw[:].rearrange("p a (b m t) -> p (a b) t m", t=PACK, m=P),
@@ -155,8 +155,9 @@ def tile_list_essay_mark_moderation_kernel(
             grouped = slot([P, PACK, P, PACK], BF16, f"w1_grouped{b}{a}", f"grouped{a}")
             dst = grouped[:].rearrange("p t m i -> p m i t")
             src = w1_raw[b, a][:].rearrange("p i (m t) -> p m i t", t=PACK)
-            nc.vector.tensor_copy(out=dst[:, 0:share], in_=src[:, 0:share])
-            nc.scalar.copy(out=dst[:, share:P], in_=src[:, share:P])
+            for t in range(0, PACK, 2):
+                nc.vector.tensor_copy(out=dst[:, 0:share, :, t : t + 2], in_=src[:, 0:share, :, t : t + 2])
+                nc.scalar.copy(out=dst[:, share:P, :, t : t + 2], in_=src[:, share:P, :, t : t + 2])
             words = keep.tile([P, KP], U32, name=f"w1_w{b}{a}", align_bytes=64)
             sc = keep.tile([P, KP], U8, name=f"w1_sc{b}{a}", align_bytes=64)
             nc.vector.quantize_mx(
@@ -210,21 +211,15 @@ def tile_list_essay_mark_moderation_kernel(
 
         h_w, h_sc = {}, {}
 
-        def quantize_h(jh, wovens, tag, whole=None):
-            words = slot([P, passes, NJ], U32, f"h_w{jh}", tag)
-            sc = keep.tile([P, passes, NJ], U8, name=f"h_sc{jh}", align_bytes=64)
-            if whole is not None:
-                nc.vector.quantize_mx(
-                    out=words[:].rearrange("p b n -> p (b n)").bitcast(FP8X4),
-                    scales=sc[:].rearrange("p b n -> p (b n)"),
-                    in_=whole[:].rearrange("p b n t -> p (b n t)"),
-                )
-            for b in range(passes if whole is None else 0):
-                nc.vector.quantize_mx(
-                    out=words[:, b, :].bitcast(FP8X4), scales=sc[:, b, :],
-                    in_=wovens[b][:].rearrange("p n t -> p (n t)"),
-                )
-            h_w[jh], h_sc[jh] = words, sc
+        def new_h(jh, tag):
+            h_w[jh] = slot([P, passes, NJ], U32, f"h_w{jh}", tag)
+            h_sc[jh] = keep.tile([P, passes, NJ], U8, name=f"h_sc{jh}", align_bytes=64)
+
+        def quantize_h(jh, b, woven):
+            nc.vector.quantize_mx(
+                out=h_w[jh][:, b, :].bitcast(FP8X4), scales=h_sc[jh][:, b, :],
+                in_=woven[:].rearrange("p n t -> p (n t)"),
+            )
 
         v2_w = []
         v2_sc = keep.tile([P, S2], U8, name="v2_sc", align_bytes=64)
@@ -288,7 +283,9 @@ def tile_list_essay_mark_moderation_kernel(
                 out=pages[c][:].indirect(cut), in0=marks[c, jh][:], in1=wgo_sb[jh][:], op=ALU.mult
             )
             if jh == halves - 1:
-                nc.sync.dma_start(out=out[c * P : (c + 1) * P, :], in_=pages[c][:])
+                rows = out[c * P : (c + 1) * P, :]
+                nc.sync.dma_start(out=rows[:, 0 : T2 // 2], in_=pages[c][:, 0 : T2 // 2])
+                nc.sync.dma_start(out=rows[:, T2 // 2 : T2], in_=pages[c][:, T2 // 2 : T2])
 
         gather_scripts(0)
         gather_scripts(1)
@@ -313,9 +310,11 @@ def tile_list_essay_mark_moderation_kernel(
         for t in range(PACK):
             bend(1, 0, t, 4 + t, bent[:, t, :])
             join(1, t, planes10, bent[:, t, :], lin10[t])
+        new_h(0, "raw00")
+        quantize_h(0, 0, woven00)
         woven10 = slot([P, NJ, PACK], BF16, "woven10", "grouped1")
         weave(planes10, woven10[:], H_VECTOR_SHARE)
-        quantize_h(0, [woven00, woven10], "raw00")
+        quantize_h(0, 1, woven10)
 
         bent01 = slot([P, PACK, NJ], F32, "bent01", "tab2_w1")
         lin01 = [linear(0, 1, t, t) for t in range(PACK)]
@@ -323,9 +322,11 @@ def tile_list_essay_mark_moderation_kernel(
             bend(0, 1, t, 4 + t, bent01[:, t, :])
         score_on_vector(0, 0, match(0, 0, 4), "marks0")
         e10 = match(1, 0, 5)
-        bent11 = slot([P, PACK, NJ], F32, "bent11", "raw10")
+        bent11 = slot([P, PACK - 1, NJ], F32, "bent11", "raw10")
+        bent11_last = slot([P, NJ], F32, "bent11_last", "bent_last")
+        bents11 = [bent11[:, t, :] for t in range(PACK - 1)] + [bent11_last[:]]
         for t in range(PACK):
-            bend(1, 1, t, 6 + t % 2, bent11[:, t, :])
+            bend(1, 1, t, 6 + t % 2, bents11[t])
         back20 = score_on_tensor(2, 0, (4, 6, 7))
         planes01 = slot([P, PACK, NJ], BF16, "planes01", "grouped1")
         for t in range(PACK):
@@ -335,17 +336,23 @@ def tile_list_essay_mark_moderation_kernel(
         woven1 = slot([P, passes, NJ, PACK], BF16, "woven1", "tab2_w0")
         weave(planes01, woven1[:, 0], 0)
         planes11 = slot([P, PACK, NJ], BF16, "planes11", "marks0")
-        for t in range(PACK):
-            join(1, t, planes11, bent11[:, t, :], lin11[t])
+        for t in range(PACK - 1):
+            join(1, t, planes11, bents11[t], lin11[t])
         score_on_vector(1, 0, e10, "raw10")
+        join(1, PACK - 1, planes11, bents11[PACK - 1], lin11[PACK - 1])
         put(1, 0)
         weave(planes11, woven1[:, 1], 0)
         fetch_marks(2, 0, back20, "marks0")
-        quantize_h(1, None, "raw10", woven1)
+        new_h(1, "raw10")
+        nc.vector.quantize_mx(
+            out=h_w[1][:].rearrange("p b n -> p (b n)").bitcast(FP8X4),
+            scales=h_sc[1][:].rearrange("p b n -> p (b n)"),
+            in_=woven1[:].rearrange("p b n t -> p (b n t)"),
+        )
         fetch_marks(3, 0, score_on_tensor(3, 0, (0, 1, 2)), "marks3")
         put(2, 0)
+        score_on_vector(0, 1, match(0, 1, 5), "marks0")
         put(3, 0)
-        score_on_vector(0, 1, match(0, 1, 5), "marks3")
         fetch_marks(1, 1, score_on_tensor(1, 1, (3, 4, 6)), "raw11")
         put(0, 1)
         fetch_marks(2, 1, score_on_tensor(2, 1, (4, 0, 1)), "grouped0")

@@ -71,12 +71,11 @@ def tile_list_essay_mark_moderation_kernel(
             nc.sync.dma_start(out=tab_sc[r:P:16].bitcast(I32), in_=tab_rows[r])
         tab_w = [keep.tile([P, T], I32, name=f"tab_w{a}", align_bytes=64) for a in range(passes)]
         tab_src = [tab_words[a].rearrange("p t i -> p (t i)").bitcast(I32) for a in range(passes)]
-        nc.sync.dma_start(out=tab_w[0][:, 0 : T // 2], in_=tab_src[0][:, 0 : T // 2])
+        nc.sync.dma_start(out=tab_w[0][:], in_=tab_src[0])
         for r in range(4):
-            nc.sync.dma_start(out=w4_sc_raw[r:P:32].bitcast(I32), in_=w4_rows[r])
-        nc.sync.dma_start(out=tab_w[0][:, T // 2 : T], in_=tab_src[0][:, T // 2 : T])
+            nc.gpsimd.dma_start(out=w4_sc_raw[r:P:32].bitcast(I32), in_=w4_rows[r])
         for q in range(4):
-            nc.sync.dma_start(
+            nc.gpsimd.dma_start(
                 out=tab2_sc[32 * q + 8 : 32 * q + 16, :].bitcast(I32),
                 in_=tab2_scales.bitcast(I32)[:, 4 * q : 4 * q + 4, :],
             )
@@ -155,9 +154,8 @@ def tile_list_essay_mark_moderation_kernel(
             grouped = slot([P, PACK, P, PACK], BF16, f"w1_grouped{b}{a}", f"grouped{a}")
             dst = grouped[:].rearrange("p t m i -> p m i t")
             src = w1_raw[b, a][:].rearrange("p i (m t) -> p m i t", t=PACK)
-            for t in range(0, PACK, 2):
-                nc.vector.tensor_copy(out=dst[:, 0:share, :, t : t + 2], in_=src[:, 0:share, :, t : t + 2])
-                nc.scalar.copy(out=dst[:, share:P, :, t : t + 2], in_=src[:, share:P, :, t : t + 2])
+            nc.vector.tensor_copy(out=dst[:, 0:share], in_=src[:, 0:share])
+            nc.scalar.copy(out=dst[:, share:P], in_=src[:, share:P])
             words = keep.tile([P, KP], U32, name=f"w1_w{b}{a}", align_bytes=64)
             sc = keep.tile([P, KP], U8, name=f"w1_sc{b}{a}", align_bytes=64)
             nc.vector.quantize_mx(
@@ -332,6 +330,7 @@ def tile_list_essay_mark_moderation_kernel(
         for t in range(PACK):
             join(0, t, planes01, bent01[:, t, :], lin01[t])
         lin11 = [linear(1, 1, t, t) for t in range(PACK)]
+        fetch_marks(3, 0, score_on_tensor(3, 0, (4, 6, 4)), "marks3")
         put(0, 0)
         woven1 = slot([P, passes, NJ, PACK], BF16, "woven1", "tab2_w0")
         weave(planes01, woven1[:, 0], 0)
@@ -349,14 +348,13 @@ def tile_list_essay_mark_moderation_kernel(
             scales=h_sc[1][:].rearrange("p b n -> p (b n)"),
             in_=woven1[:].rearrange("p b n t -> p (b n t)"),
         )
-        fetch_marks(3, 0, score_on_tensor(3, 0, (0, 1, 2)), "marks3")
         put(2, 0)
-        score_on_vector(0, 1, match(0, 1, 5), "marks0")
+        fetch_marks(0, 1, score_on_tensor(0, 1, (5, 0, 1)), "bent_last")
         put(3, 0)
-        fetch_marks(1, 1, score_on_tensor(1, 1, (3, 4, 6)), "raw11")
+        fetch_marks(1, 1, score_on_tensor(1, 1, (5, 2, 3)), "raw11")
         put(0, 1)
-        fetch_marks(2, 1, score_on_tensor(2, 1, (4, 0, 1)), "grouped0")
+        fetch_marks(2, 1, score_on_tensor(2, 1, (5, 0, 1)), "grouped0")
         put(1, 1)
-        fetch_marks(3, 1, score_on_tensor(3, 1, (0, 3, 6)), "planes0")
+        fetch_marks(3, 1, score_on_tensor(3, 1, (5, 2, 3)), "planes0")
         put(2, 1)
         put(3, 1)

from contextlib import ExitStack

import concourse.mybir as mybir
from concourse.masks import make_identity

K, H, T, S, T2, T3, S2 = 1024, 1024, 4096, 1024, 2048, 2048, 512
FLOPS = 2 * (2 * K * H * S + H * S2 * S)

F32 = mybir.dt.float32
BF16 = mybir.dt.bfloat16
I32 = mybir.dt.int32
U32 = mybir.dt.uint32
U16 = mybir.dt.uint16
U8 = mybir.dt.uint8
FP8X4 = mybir.dt.float8_e4m3fn_x4
FP4X4 = mybir.dt.float4_e2m1fn_x4
ALU = mybir.AluOpType
ACT = mybir.ActivationFunctionType

P = 128
PACK = 4
KP = P * PACK
NJ = 512
W1_VECTOR_SHARE = 80
H_VECTOR_SHARE = 320


def tile_list_essay_mark_moderation_kernel(
    tc, tab_words, tab_scales, offs, w1, gain, w4_words, w4_scales,
    tab2_words, tab2_scales, offs2, aw, prior, page1, wgo, offs3, out,
):
    nc = tc.nc
    passes = K // KP
    halves = S // NJ
    row_tiles = S2 // P
    list_cols = NJ // 16

    with ExitStack() as ctx:
        keep = ctx.enter_context(tc.tile_pool(name="keep", bufs=1))
        ring = ctx.enter_context(tc.tile_pool(name="ring", bufs=1))
        psum = ctx.enter_context(tc.psum_pool(name="psum", bufs=1))

        idx = keep.tile([P, S // 16], U16, name="idx")
        idx2 = keep.tile([P, S2 // 16], U16, name="idx2")
        idx3 = keep.tile([P, S // 16], U16, name="idx3")

        def slot(shape, dtype, name, tag):
            return ring.tile(shape, dtype, name=name, tag=tag, bufs=1, align_bytes=64)

        def bank(n, name):
            return psum.tile([P, NJ], F32, name=name, tag=f"bank{n}")

        tab_sc = keep.tile([P, T], U8, name="tab_sc", align_bytes=64)
        w4_sc_raw = keep.tile([P, passes, H], U8, name="w4_sc_raw", align_bytes=64)
        tab2_sc = keep.tile([P, T3], U8, name="tab2_sc", align_bytes=64)
        v_sc_moved = keep.tile([P, S], U8, name="v_sc_moved", align_bytes=64)
        nc.vector.memset(tab_sc[:, 0 : T // 2].bitcast(I32), 0)
        nc.gpsimd.memset(tab_sc[:, T // 2 : T].bitcast(I32), 0)
        nc.gpsimd.memset(v_sc_moved[:].bitcast(I32), 0)
        nc.vector.memset(w4_sc_raw[:].bitcast(I32), 0)
        nc.vector.memset(tab2_sc[:].bitcast(I32), 0)
        tab_rows = tab_scales.bitcast(I32).rearrange("a (q r) t -> r q a t", r=4)
        w4_rows = w4_scales.bitcast(I32).rearrange("a (q r) t -> r q a t", r=4)

        nc.sync.dma_start(idx[:], offs)
        gain_sb = keep.tile([P, passes, PACK], F32, name="gain_sb")
        nc.sync.dma_start(idx2[:], offs2)
        w4_raw = keep.tile([P, passes, 2 * H], U8, name="w4_raw", align_bytes=64)
        nc.sync.dma_start(out=w4_raw[:].bitcast(I32), in_=w4_words.bitcast(I32).rearrange("a p c -> p a c"))
        for r in range(4):
            nc.sync.dma_start(out=tab_sc[r:P:16].bitcast(I32), in_=tab_rows[r])
        tab_w = [keep.tile([P, T], I32, name=f"tab_w{a}", align_bytes=64) for a in range(passes)]
        tab_src = [tab_words[a].rearrange("p t i -> p (t i)").bitcast(I32) for a in range(passes)]
        nc.sync.dma_start(out=tab_w[0][:], in_=tab_src[0])
        for r in range(4):
            nc.gpsimd.dma_start(out=w4_sc_raw[r:P:32].bitcast(I32), in_=w4_rows[r])
        for q in range(4):
            nc.gpsimd.dma_start(
                out=tab2_sc[32 * q + 8 : 32 * q + 16, :].bitcast(I32),
                in_=tab2_scales.bitcast(I32)[:, 4 * q : 4 * q + 4, :],
            )
        nc.sync.dma_start(out=tab_w[1][:], in_=tab_src[1])
        nc.sync.dma_start(out=gain_sb[:], in_=gain.rearrange("(b p t) -> p b t", p=P, t=PACK))
        w1_raw = {}
        for b in range(passes):
            for a in range(passes):
                raw = slot([P, PACK, KP], F32, f"w1_raw{b}{a}", f"raw{b}{a}")
                nc.sync.dma_start(
                    out=raw[:],
                    in_=w1[a * KP : (a + 1) * KP, b * KP : (b + 1) * KP].rearrange("(p i) c -> p i c", i=PACK),
                )
                w1_raw[b, a] = raw
        tab2_w = []
        for b in range(passes):
            tw = slot([P, T3], I32, f"tab2_w{b}", f"tab2_w{b}")
            nc.sync.dma_start(out=tw[:], in_=tab2_words[b].rearrange("p t i -> p (t i)").bitcast(I32))
            tab2_w.append(tw)
        nc.sync.dma_start(idx3[:], offs3)
        aw_sb = keep.tile([P, row_tiles], F32, name="aw_sb")
        with nc.allow_non_contiguous_dma(reason="one anchor weight for each partition and row tile"):
            nc.sync.dma_start(out=aw_sb[:], in_=aw.rearrange("(c p) -> p c", p=P))
        wgo_sb = [keep.tile([P, NJ], F32, name=f"wgo{jh}") for jh in range(halves)]
        nc.sync.dma_start(out=wgo_sb[0][:], in_=wgo[:, 0:NJ])
        prior_sb = {}

        def load_prior(jh, tag):
            pr = slot([P, row_tiles, NJ], F32, f"prior{jh}", tag)
            nc.sync.dma_start(
                out=pr[:], in_=prior[:, jh * NJ : (jh + 1) * NJ].rearrange("(c p) n -> p c n", p=P)
            )
            prior_sb[jh] = pr

        load_prior(0, "prior0")
        pages = []
        for c in range(row_tiles):
            page = keep.tile([P, T2], F32, name=f"page{c}")
            nc.sync.dma_start(out=page[:], in_=page1[c * P : (c + 1) * P, :])
            pages.append(page)
        nc.sync.dma_start(out=wgo_sb[1][:], in_=wgo[:, NJ : 2 * NJ])

        ident = keep.tile([P, P], F32, name="ident")
        make_identity(nc, ident[:])

        v_sc_packed = keep.tile([P, S], U8, name="v_sc_packed", align_bytes=64)
        nc.vector.tensor_copy(out=v_sc_packed[:], in_=tab_sc[:].indirect(idx[:]))
        nc.gpsimd.dma_start(out=v_sc_moved[0 : P - 16, :].bitcast(I32), in_=v_sc_packed[16:P, :].bitcast(I32))
        w4_w = keep.tile([P, passes, 2 * H], U8, name="w4_w", align_bytes=64)
        w4_sc = keep.tile([P, passes, H], U8, name="w4_sc", align_bytes=64)
        w4_dst = w4_w[:].bitcast(U16).rearrange("p a (b t m) -> p (a b) m t", t=PACK, m=P)
        w4_src = w4_raw[:].bitcast(U16).rearrange("p a (b m t) -> p (a b) m t", t=PACK, m=P)
        for t in range(0, PACK, 2):
            nc.scalar.copy(out=w4_dst[:, :, :, t : t + 2], in_=w4_src[:, :, :, t : t + 2])
        nc.vector.tensor_copy(
            out=w4_sc[:].rearrange("p a (b t m) -> p (a b) t m", t=PACK, m=P),
            in_=w4_sc_raw[:].rearrange("p a (b m t) -> p (a b) t m", t=PACK, m=P),
        )

        v_w = {}
        v_sc = {
            (a, jh): (v_sc_packed, v_sc_moved)[a][:, jh * NJ : (jh + 1) * NJ]
            for a in range(passes) for jh in range(halves)
        }

        def gather_scripts(jh):
            cut = idx[:, jh * list_cols : (jh + 1) * list_cols]
            for a in range(passes):
                words = keep.tile([P, NJ], U32, name=f"v_w{a}{jh}", align_bytes=64)
                nc.vector.tensor_copy(out=words[:], in_=tab_w[a][:].bitcast(U32).indirect(cut))
                v_w[a, jh] = words

        w1_w, w1_sc = {}, {}

        def quantize_w1(b, a, share):
            grouped = slot([P, PACK, P, PACK], BF16, f"w1_grouped{b}{a}", f"grouped{a}")
            dst = grouped[:].rearrange("p t m i -> p m i t")
            src = w1_raw[b, a][:].rearrange("p i (m t) -> p m i t", t=PACK)
            nc.vector.tensor_copy(out=dst[:, 0:share], in_=src[:, 0:share])
            nc.scalar.copy(out=dst[:, share:P], in_=src[:, share:P])
            words = keep.tile([P, KP], U32, name=f"w1_w{b}{a}", align_bytes=64)
            sc = keep.tile([P, KP], U8, name=f"w1_sc{b}{a}", align_bytes=64)
            nc.vector.quantize_mx(
                out=words[:].bitcast(FP8X4), scales=sc[:], in_=grouped[:].rearrange("p t m i -> p (t m i)")
            )
            w1_w[b, a], w1_sc[b, a] = words, sc

        def linear(b, jh, t, n):
            lin = bank(n, f"lin{b}{jh}")
            c0 = b * KP + t * P
            for a in range(passes):
                nc.tensor.matmul_mx(
                    out=lin[:],
                    lhsT=w4_w[:, a, 2 * c0 : 2 * (c0 + P)].bitcast(FP4X4),
                    lhsT_scale=w4_sc[:, a, c0 : c0 + P],
                    rhs=v_w[a, jh][:].bitcast(FP8X4),
                    rhs_scale=v_sc[a, jh],
                    start=(a == 0), stop=(a == passes - 1),
                )
            return lin

        def bend(b, jh, t, n, bent):
            pre = bank(n, f"pre{b}{jh}")
            for a in range(passes):
                nc.tensor.matmul_mx(
                    out=pre[:],
                    lhsT=w1_w[b, a][:, t * P : (t + 1) * P].bitcast(FP8X4),
                    lhsT_scale=w1_sc[b, a][:, t * P : (t + 1) * P],
                    rhs=v_w[a, jh][:].bitcast(FP8X4),
                    rhs_scale=v_sc[a, jh],
                    start=(a == 0), stop=(a == passes - 1),
                )
            nc.scalar.activation(out=bent, in_=pre[:], func=ACT.Tanh)

        def join(b, t, planes, bent, lin):
            nc.vector.scalar_tensor_tensor(
                out=planes[:, t, :], in0=bent, scalar=gain_sb[:, b, t : t + 1], in1=lin[:],
                op0=ALU.mult, op1=ALU.add,
            )

        def weave(planes, woven, vector_cols):
            dst = woven.rearrange("p (g n) t -> p g t n", n=4)
            src = planes[:].rearrange("p t (g n) -> p g t n", n=4)
            cut = vector_cols // 4
            if cut > 0:
                nc.vector.tensor_copy(out=dst[:, 0:cut], in_=src[:, 0:cut])
                nc.scalar.copy(out=dst[:, cut : NJ // 4], in_=src[:, cut : NJ // 4])
            else:
                nc.scalar.copy(out=dst[:, 0 : NJ // 8], in_=src[:, 0 : NJ // 8])
                nc.scalar.copy(out=dst[:, NJ // 8 : NJ // 4], in_=src[:, NJ // 8 : NJ // 4])

        h_w, h_sc = {}, {}

        def new_h(jh, tag):
            h_w[jh] = slot([P, passes, NJ], U32, f"h_w{jh}", tag)
            h_sc[jh] = keep.tile([P, passes, NJ], U8, name=f"h_sc{jh}", align_bytes=64)

        def quantize_h(jh, b, woven):
            nc.vector.quantize_mx(
                out=h_w[jh][:, b, :].bitcast(FP8X4), scales=h_sc[jh][:, b, :],
                in_=woven[:].rearrange("p n t -> p (n t)"),
            )

        v2_w = []
        v2_sc = keep.tile([P, S2], U8, name="v2_sc", align_bytes=64)

        def gather_anchors():
            for b in range(passes):
                words = keep.tile([P, S2], U32, name=f"v2_w{b}", align_bytes=64)
                nc.vector.tensor_copy(out=words[:], in_=tab2_w[b][:].bitcast(U32).indirect(idx2[:]))
                v2_w.append(words)

        marks = {}

        def match(c, jh, n):
            e = bank(n, f"e{c}{jh}")
            for b in range(passes):
                nc.tensor.matmul_mx(
                    out=e[:],
                    lhsT=v2_w[b][:, c * P : (c + 1) * P].bitcast(FP8X4),
                    lhsT_scale=v2_sc[8 + 4 * b : P, c * P : (c + 1) * P],
                    rhs=h_w[jh][:, b, :].bitcast(FP8X4),
                    rhs_scale=h_sc[jh][:, b, :],
                    start=(b == 0), stop=(b == passes - 1),
                )
            return e

        def score_on_vector(c, jh, e, tag):
            mk = slot([P, NJ], F32, f"marks{c}{jh}", tag)
            nc.vector.scalar_tensor_tensor(
                out=mk[:], in0=e[:], scalar=aw_sb[:, c : c + 1], in1=prior_sb[jh][:, c, :],
                op0=ALU.mult, op1=ALU.add,
            )
            marks[c, jh] = mk

        def score_on_tensor(c, jh, banks):
            e = match(c, jh, banks[0])
            scaled = slot([P, NJ], F32, f"scaled{c}{jh}", f"scaled{c % 2}")
            nc.scalar.activation(out=scaled[:], in_=e[:], func=ACT.Copy, scale=aw_sb[:, c : c + 1])
            turned = bank(banks[1], f"turned{c}{jh}")
            for g in range(NJ // P):
                cols = slice(g * P, (g + 1) * P)
                nc.tensor.matmul(turned[:, cols], lhsT=prior_sb[jh][:, c, cols], rhs=ident[:],
                                 is_transpose=True, start=True, stop=False)
                nc.tensor.matmul(turned[:, cols], lhsT=scaled[:, cols], rhs=ident[:],
                                 is_transpose=True, start=False, stop=True)
            summed = slot([P, NJ], F32, f"summed{c}{jh}", f"summed{c % 2}")
            nc.scalar.copy(out=summed[:], in_=turned[:])
            back = bank(banks[2], f"back{c}{jh}")
            for g in range(NJ // P):
                cols = slice(g * P, (g + 1) * P)
                nc.tensor.transpose(back[:, cols], summed[:, cols], ident[:])
            return back

        def fetch_marks(c, jh, back, tag):
            mk = slot([P, NJ], F32, f"marks{c}{jh}", tag)
            nc.scalar.copy(out=mk[:], in_=back[:])
            marks[c, jh] = mk

        def put(c, jh):
            cut = idx3[:, jh * list_cols : (jh + 1) * list_cols]
            nc.vector.tensor_tensor(
                out=pages[c][:].indirect(cut), in0=marks[c, jh][:], in1=wgo_sb[jh][:], op=ALU.mult
            )
            if jh == halves - 1:
                rows = out[c * P : (c + 1) * P, :]
                nc.sync.dma_start(out=rows[:, 0 : T2 // 2], in_=pages[c][:, 0 : T2 // 2])
                nc.sync.dma_start(out=rows[:, T2 // 2 : T2], in_=pages[c][:, T2 // 2 : T2])

        gather_scripts(0)
        gather_scripts(1)
        nc.vector.tensor_copy(out=v2_sc[:], in_=tab2_sc[:].indirect(idx2[:]))
        lin00 = [linear(0, 0, t, t) for t in range(PACK)]
        quantize_w1(0, 0, 80)
        quantize_w1(0, 1, 80)
        quantize_w1(1, 0, 80)
        load_prior(1, "raw01")
        planes00 = slot([P, PACK, NJ], BF16, "planes00", "planes0")
        bent = slot([P, PACK, NJ], F32, "bent00", "raw10")
        for t in range(PACK):
            bend(0, 0, t, 4 + t, bent[:, t, :])
            join(0, t, planes00, bent[:, t, :], lin00[t])
        lin10 = [linear(1, 0, t, t) for t in range(PACK)]
        quantize_w1(1, 1, 80)
        woven00 = slot([P, NJ, PACK], BF16, "woven00", "grouped0")
        weave(planes00, woven00[:], 0)
        gather_anchors()
        planes10 = slot([P, PACK, NJ], BF16, "planes10", "tab2_w1")
        bent = slot([P, PACK, NJ], F32, "bent10", "raw00")
        for t in range(PACK):
            bend(1, 0, t, 4 + t, bent[:, t, :])
            join(1, t, planes10, bent[:, t, :], lin10[t])
        new_h(0, "raw00")
        quantize_h(0, 0, woven00)
        woven10 = slot([P, NJ, PACK], BF16, "woven10", "grouped1")
        weave(planes10, woven10[:], H_VECTOR_SHARE)
        quantize_h(0, 1, woven10)

        bent01 = slot([P, PACK, NJ], F32, "bent01", "tab2_w1")
        lin01 = [linear(0, 1, t, t) for t in range(PACK)]
        for t in range(PACK):
            bend(0, 1, t, 4 + t, bent01[:, t, :])
        score_on_vector(0, 0, match(0, 0, 4), "marks0")
        e10 = match(1, 0, 5)
        bent11 = slot([P, PACK - 1, NJ], F32, "bent11", "raw10")
        bent11_last = slot([P, NJ], F32, "bent11_last", "bent_last")
        bents11 = [bent11[:, t, :] for t in range(PACK - 1)] + [bent11_last[:]]
        for t in range(PACK):
            bend(1, 1, t, 6 + t % 2, bents11[t])
        back20 = score_on_tensor(2, 0, (4, 6, 7))
        planes01 = slot([P, PACK, NJ], BF16, "planes01", "grouped1")
        for t in range(PACK):
            join(0, t, planes01, bent01[:, t, :], lin01[t])
        lin11 = [linear(1, 1, t, t) for t in range(PACK)]
        fetch_marks(3, 0, score_on_tensor(3, 0, (4, 6, 4)), "marks3")
        put(0, 0)
        woven1 = slot([P, passes, NJ, PACK], BF16, "woven1", "tab2_w0")
        weave(planes01, woven1[:, 0], 0)
        planes11 = slot([P, PACK, NJ], BF16, "planes11", "marks0")
        for t in range(PACK - 1):
            join(1, t, planes11, bents11[t], lin11[t])
        score_on_vector(1, 0, e10, "raw10")
        join(1, PACK - 1, planes11, bents11[PACK - 1], lin11[PACK - 1])
        put(1, 0)
        weave(planes11, woven1[:, 1], 0)
        fetch_marks(2, 0, back20, "marks0")
        new_h(1, "raw10")
        nc.vector.quantize_mx(
            out=h_w[1][:].rearrange("p b n -> p (b n)").bitcast(FP8X4),
            scales=h_sc[1][:].rearrange("p b n -> p (b n)"),
            in_=woven1[:].rearrange("p b n t -> p (b n t)"),
        )
        put(2, 0)
        fetch_marks(0, 1, score_on_tensor(0, 1, (5, 0, 1)), "bent_last")
        put(3, 0)
        fetch_marks(1, 1, score_on_tensor(1, 1, (5, 2, 3)), "raw11")
        put(0, 1)
        fetch_marks(2, 1, score_on_tensor(2, 1, (5, 0, 1)), "grouped0")
        put(1, 1)
        fetch_marks(3, 1, score_on_tensor(3, 1, (5, 2, 3)), "planes0")
        put(2, 1)
        put(3, 1)
